import numpy as np
import ml_dtypes


def mxq(x, axis, fmt="e4m3"):
    dtype, down = {"e4m3": (ml_dtypes.float8_e4m3fn, 7), "e5m2": (ml_dtypes.float8_e5m2, 14)}[fmt]
    v = np.moveaxis(np.asarray(x, np.float32).astype(ml_dtypes.bfloat16).astype(np.float64), axis, -1)
    blocks = v.reshape(v.shape[:-1] + (-1, 32))
    amax = np.abs(blocks).max(-1, keepdims=True)
    byte = np.maximum(np.where(amax > 0, np.frexp(amax)[1] - 1 + 127, 0) - down, 1)
    scale = np.exp2(byte - 127.0)
    codes = (blocks / scale).astype(np.float32).astype(dtype).astype(np.float64)
    return np.moveaxis((codes * scale).reshape(v.shape), -1, axis)


WIDE = False


def mx_kscale(k):
    if not WIDE:
        return np.ones(k)
    levels = np.array([10, -10, 5, -5, 0])
    if k % 512:
        return np.exp2(np.random.permutation(np.resize(levels, k // 32))).repeat(32)
    a = np.empty((k // 512, 16))
    for p in range(k // 512):
        a[p, :8] = np.random.permutation(np.resize(levels, 8))
        for g in range(8):
            far = levels[np.abs(levels - a[p, g]) >= 10]
            a[p, g + 8] = far[np.random.randint(len(far))]
    return np.exp2(a.ravel()).repeat(32)


def f64(x):
    return np.asarray(x).astype(np.float64)


def striped(idx):
    return np.tile(idx.reshape(-1, 16).T, (8, 1)).astype(np.uint16)


def unstriped(offs):
    return offs[:16].T.reshape(-1).astype(np.int64)


def striped8(idx):
    return np.concatenate([x.reshape(-1, 16).T for x in idx]).astype(np.uint16)


def runs(offs, k):
    lists = np.stack([offs[16 * r : 16 * r + 16].T.reshape(-1) for r in range(8)]).astype(np.int64)
    return lists[np.arange(k) % 512 // 64]


def pack_weight(w):
    k, n = w.shape
    w = f64(np.asarray(w, np.float32).astype(ml_dtypes.bfloat16)).reshape(k // 32, 32, n)
    amax = np.abs(w).max(1)
    byte = np.clip(np.where(amax > 0, np.frexp(amax)[1] - 1 + 127 - 7, 1), 1, 254)
    scaled = (w * np.exp2(127.0 - byte)[:, None, :]).reshape(k, n).astype(np.float32)
    words = np.ascontiguousarray(scaled.reshape(k // 512, 128, 4, n).transpose(0, 1, 3, 2)).astype(ml_dtypes.float8_e4m3fn).view(np.uint8)
    return words, np.ascontiguousarray(byte.astype(np.uint8).reshape(k // 512, 16, n))


def unpack_weight(words, scales):
    g, p, n, _ = words.shape
    vals = np.ascontiguousarray(words).view(ml_dtypes.float8_e4m3fn).astype(np.float64) * np.repeat(np.exp2(scales.astype(np.float64) - 127.0), 8, axis=1)[..., None]
    return vals.transpose(0, 1, 3, 2).reshape(g * 512, n)


def sigmoid(v):
    return 1.0 / (1.0 + np.exp(-np.maximum(v, -700.0)))


K, T, S, N, H = 512, 2048, 512, 512, 512


def setup_inputs():
    n = np.random.standard_normal
    s = mx_kscale(K)[:, None]
    u = mx_kscale(S)
    packed_xT = pack_weight(n((K, T)) * s)
    return {
        "x_words": packed_xT[0],
        "x_scales": packed_xT[1],
        "wa": (n((K, H)) / np.sqrt(K) / s).astype(np.float32),
        "gt": (np.random.uniform(0.5, 1.5, (S, 1)) * u[:, None]).astype(np.float32),
        "w1": (n((S, N)) / np.sqrt(S) / u[:, None]).astype(np.float32),
        "offs": striped(np.random.permutation(T)[:S]),
        "n1": striped8(np.stack([np.random.permutation(H) for _ in range(8)])),
        "n2": striped8(np.stack([np.random.permutation(H) for _ in range(8)])),
        "n3": striped8(np.stack([np.random.permutation(H) for _ in range(8)])),
        "n4": striped8(np.stack([np.random.permutation(H) for _ in range(8)])),
        "n5": striped8(np.stack([np.random.permutation(H) for _ in range(8)])),
    }


def reference(x_words, x_scales, wa, gt, w1, offs, n1, n2, n3, n4, n5):
    xq = unpack_weight(x_words, x_scales)[:, unstriped(offs)]
    y = xq.T @ mxq(f64(wa), 0, "e4m3")
    z = f64(gt) * (0.75 * (y[np.arange(S)[:, None], runs(n1, S)] + y[np.arange(S)[:, None], runs(n2, S)]) - y)
    h = mxq(f64(w1), 0, "e4m3").T @ mxq(z, 0, "e4m3")
    return (h[np.arange(N)[:, None], runs(n3, N)]) * sigmoid(h) + (h[np.arange(N)[:, None], runs(n4, N)]) * (sigmoid(h[np.arange(N)[:, None], runs(n5, N)]))

@@ -1,0 +1,213 @@
+from contextlib import ExitStack
+
+import concourse.mybir as mybir
+
+K, T, S, N, H = 512, 2048, 512, 512, 512
+FLOPS = 2 * K * S * H + 2 * S * N * H
+
+F32 = mybir.dt.float32
+BF16 = mybir.dt.bfloat16
+I32 = mybir.dt.int32
+U32 = mybir.dt.uint32
+U16 = mybir.dt.uint16
+U8 = mybir.dt.uint8
+FP8X4 = mybir.dt.float8_e4m3fn_x4
+ALU = mybir.AluOpType
+ACT = mybir.ActivationFunctionType
+
+P = 128
+PACK = 4
+HALVES = 2
+W = H // HALVES
+LIST_COLS = W // 16
+
+
+def tile_picked_toklapwsum_none_p_kernel(
+    tc, x_words, x_scales, wa, gt, w1, offs, n1, n2, n3, n4, n5, out
+):
+    nc = tc.nc
+    with ExitStack() as ctx:
+        held = ctx.enter_context(tc.tile_pool(name="held", bufs=1))
+        psum = ctx.enter_context(tc.psum_pool(name="psum", bufs=8))
+
+        def sbuf(name, shape, dtype):
+            return held.tile(shape, dtype, name=name, align_bytes=64)
+
+        def load_list(name, source):
+            tile = held.tile([P, S // 16], U16, name=name)
+            nc.sync.dma_start(tile[:], source)
+            return tile
+
+        def half(h):
+            return slice(h * W, (h + 1) * W)
+
+        def entries(tile, h):
+            return tile[:, h * LIST_COLS : (h + 1) * LIST_COLS]
+
+        def interleave(copy, grouped, planes):
+            copy(
+                grouped.rearrange("p (c i) j -> p c j i", i=4),
+                planes.rearrange("p j (c i) -> p c j i", i=4),
+            )
+
+        def quantize(name, grouped, width):
+            codes = sbuf(name + "_codes", [P, width], U32)
+            scales = sbuf(name + "_scales", [P, width], U8)
+            nc.vector.quantize_mx(out=codes[:].bitcast(FP8X4), scales=scales[:], in_=grouped)
+            return codes, scales
+
+        def product(name, lhs_codes, lhs_scales, rhs):
+            acc = psum.tile([P, W], F32, name=name, tag="acc")
+            nc.tensor.matmul_mx(
+                out=acc[:],
+                lhsT=lhs_codes.bitcast(FP8X4),
+                lhsT_scale=lhs_scales,
+                rhs=rhs[0][:].bitcast(FP8X4),
+                rhs_scale=rhs[1][:],
+                start=True,
+                stop=True,
+            )
+            return acc
+
+        table_scales = sbuf("table_scales", [P, T], U8)
+        nc.vector.memset(table_scales[:].bitcast(I32), 0)
+        picks = load_list("picks", offs)
+        wa_rows = wa.rearrange("(p j) n -> p j n", j=PACK)
+        wa_raw = [sbuf("wa_raw%d" % h, [P, PACK, W], F32) for h in range(HALVES)]
+        nc.sync.dma_start(wa_raw[0][:], wa_rows[:, :, half(0)])
+        for q in range(4):
+            nc.sync.dma_start(
+                table_scales[32 * q : 32 * q + 4, :].bitcast(I32), x_scales[0, 4 * q : 4 * q + 4, :].bitcast(I32)
+            )
+        table_words = sbuf("table_words", [P, T], I32)
+        nc.sync.dma_start(table_words[:], x_words[0].rearrange("p n t -> p (n t)").bitcast(I32))
+        nc.sync.dma_start(wa_raw[1][:], wa_rows[:, :, half(1)])
+        gains = sbuf("gains", [P, PACK], F32)
+        nc.sync.dma_start(gains[:], gt.rearrange("(p t) o -> p (t o)", t=PACK))
+        list1 = load_list("list1", n1)
+        list2 = load_list("list2", n2)
+        w1_raw = sbuf("w1_raw", [P, PACK, N], F32)
+        nc.sync.dma_start(w1_raw[:], w1.rearrange("(p j) n -> p j n", j=PACK))
+        list5 = load_list("list5", n5)
+        list3 = load_list("list3", n3)
+        list4 = load_list("list4", n4)
+
+        picked_scales = sbuf("picked_scales", [P, S], U8)
+        nc.vector.tensor_copy(picked_scales[:], table_scales[:].indirect(picks[:]))
+        token_scales = sbuf("token_scales", [P, PACK, P], U8)
+        nc.vector.tensor_copy(token_scales[:], picked_scales[:].rearrange("p (m t) -> p t m", t=PACK))
+        token_words = sbuf("token_words", [P, PACK, P], U32)
+        nc.vector.tensor_copy(
+            token_words[:].rearrange("p t m -> p m t"), table_words[:].bitcast(U32).indirect(picks[:])
+        )
+
+        gy = [sbuf("gy%d" % t, [P, H], F32) for t in range(PACK)]
+        y_acc = {}
+        for h in range(HALVES):
+            grouped = sbuf("wa_grouped%d" % h, [P, W, PACK], BF16)
+            if h == 0:
+                interleave(nc.scalar.copy, grouped[:], wa_raw[h][:])
+            else:
+                cut = 160
+                interleave(nc.vector.tensor_copy, grouped[:, :cut, :], wa_raw[h][:, :, :cut])
+                interleave(nc.scalar.copy, grouped[:, cut:, :], wa_raw[h][:, :, cut:])
+            wa_q = quantize("wa%d" % h, grouped[:].rearrange("p c j -> p (c j)"), W)
+            for t in range(PACK):
+                y_acc[t, h] = product("y%d_%d" % (t, h), token_words[:, t, :], token_scales[:, t, :], wa_q)
+
+        w1_grouped = sbuf("w1_grouped", [P, PACK, P, PACK], BF16)
+        half_window = [sbuf("half_window%d" % t, [P, 2 * H], F32) for t in range(PACK)]
+        tanh_window = [sbuf("tanh_window%d" % t, [P, 2 * H], F32) for t in range(PACK)]
+        half_h = [tile[:, :H] for tile in half_window]
+        tanh_h = [tile[:, :H] for tile in tanh_window]
+        firsts = {}
+
+        def weigh_on_scalar(t, h):
+            nc.scalar.activation(gy[t][:, half(h)], y_acc[t, h][:], ACT.Copy, scale=gains[:, t : t + 1])
+
+        def weigh_on_vector(t, h):
+            nc.vector.tensor_scalar(gy[t][:, half(h)], y_acc[t, h][:], gains[:, t : t + 1], None, ALU.mult)
+
+        def look_up_first(t, h):
+            first = tanh_window[t][:, H + h * W : H + (h + 1) * W]
+            nc.scalar.activation(first, gy[t][:].indirect(entries(list1, h)), ACT.Copy)
+            firsts[t, h] = first
+
+        def cast_w1():
+            for g in range(2):
+                ms = slice(g * P // 2, (g + 1) * P // 2)
+                nc.scalar.copy(
+                    w1_grouped[:, :, ms, :].rearrange("p t m j -> p m j t"),
+                    w1_raw[:].rearrange("p j (m t) -> p m j t", t=PACK)[:, ms, :, :],
+                )
+
+        z_planes = [sbuf("z_planes%d" % h, [P, PACK, W], BF16) for h in range(HALVES)]
+        z_grouped = [sbuf("z_grouped%d" % h, [P, W, PACK], BF16) for h in range(HALVES)]
+        pair_sums = {}
+
+        def add_second(t, h):
+            both = half_window[t][:, H:][:, half(h)]
+            nc.vector.tensor_tensor(both, gy[t][:].indirect(entries(list2, h)), firsts[t, h], ALU.add)
+            pair_sums[t, h] = both
+
+        def finish_z(t, h):
+            nc.vector.scalar_tensor_tensor(
+                z_planes[h][:, t, :], pair_sums[t, h], 0.75, gy[t][:, half(h)], ALU.mult, ALU.subtract
+            )
+
+        h_acc = {}
+
+        def second_product(h, z_q, w1_q):
+            for t in range(PACK):
+                cols = slice(t * P, (t + 1) * P)
+                h_acc[t, h] = product("h%d_%d" % (t, h), w1_q[0][:, cols], w1_q[1][:, cols], z_q)
+                if h == 0 or t == 0:
+                    nc.scalar.activation(tanh_h[t][:, half(h)], h_acc[t, h][:], ACT.Tanh, scale=0.5)
+
+        for t in range(PACK):
+            weigh_on_scalar(t, 0)
+            weigh_on_vector(t, 1)
+            look_up_first(t, 0)
+        for t in range(PACK):
+            look_up_first(t, 1)
+        cast_w1()
+
+        steps = [(t, h) for h in range(HALVES) for t in range(PACK)]
+        for i, step in enumerate(steps):
+            add_second(*step)
+            if i > 0:
+                finish_z(*steps[i - 1])
+        finish_z(*steps[-1])
+        interleave(nc.scalar.copy, z_grouped[0][:], z_planes[0][:])
+        w1_q = quantize("w1", w1_grouped[:].rearrange("p t m j -> p (t m j)"), N)
+        z_q0 = quantize("z0", z_grouped[0][:].rearrange("p c j -> p (c j)"), W)
+        second_product(0, z_q0, w1_q)
+        interleave(nc.vector.tensor_copy, z_grouped[1][:], z_planes[1][:])
+        z_q1 = quantize("z1", z_grouped[1][:].rearrange("p c j -> p (c j)"), W)
+        second_product(1, z_q1, w1_q)
+        for t in range(PACK):
+            for h in range(HALVES):
+                nc.vector.tensor_scalar(half_h[t][:, half(h)], h_acc[t, h][:], 0.5, None, ALU.mult)
+
+        out_rows = out.rearrange("(p t) n -> p t n", t=PACK)
+        right = sbuf("right", [P, H], F32)
+        for t in range(PACK):
+            if t > 0:
+                nc.scalar.activation(tanh_h[t][:, half(1)], half_h[t][:, half(1)], ACT.Tanh)
+            gate = sbuf("gate%d" % t, [P, H], F32)
+            third = sbuf("third%d" % t, [P, H], F32)
+            left = sbuf("left%d" % t, [P, H], F32)
+            result = sbuf("result%d" % t, [P, H], F32)
+            whole = [(slice(0, H), slice(0, H // 16))]
+            halves = [(half(h), slice(h * LIST_COLS, (h + 1) * LIST_COLS)) for h in range(HALVES)]
+            for cols, part in halves if t == PACK - 1 else whole:
+                nc.scalar.activation(gate[:, cols], tanh_window[t][:].indirect(list5[:, part]), ACT.Copy, bias=1.0)
+            for cols, part in halves if t == PACK - 1 else whole:
+                nc.vector.tensor_tensor(right[:, cols], half_window[t][:].indirect(list4[:, part]), gate[:, cols], ALU.mult)
+            for cols, part in halves if t == PACK - 1 else whole:
+                nc.scalar.activation(third[:, cols], half_window[t][:].indirect(list3[:, part]), ACT.Copy)
+                nc.vector.scalar_tensor_tensor(left[:, cols], tanh_h[t][:, cols], 1.0, third[:, cols], ALU.add, ALU.mult)
+            for cols, part in halves if t == PACK - 1 else whole:
+                nc.vector.tensor_tensor(result[:, cols], left[:, cols], right[:, cols], ALU.add)
+                nc.sync.dma_start(out_rows[:, t, cols], result[:, cols])
+            right = third

@@ -19,7 +19,7 @@ P = 128
 PACK = 4
 HALVES = 2
 W = H // HALVES
-LIST_COLS = W // 16
+WA_VECTOR_COLS = 160
 
 
 def tile_picked_toklapwsum_none_p_kernel(
@@ -41,8 +41,8 @@ def tile_picked_toklapwsum_none_p_kernel(
         def half(h):
             return slice(h * W, (h + 1) * W)
 
-        def entries(tile, h):
-            return tile[:, h * LIST_COLS : (h + 1) * LIST_COLS]
+        def entries(tile, cols):
+            return tile[:, cols.start // 16 : cols.stop // 16]
 
         def interleave(copy, grouped, planes):
             copy(
@@ -75,10 +75,8 @@ def tile_picked_toklapwsum_none_p_kernel(
         wa_rows = wa.rearrange("(p j) n -> p j n", j=PACK)
         wa_raw = [sbuf("wa_raw%d" % h, [P, PACK, W], F32) for h in range(HALVES)]
         nc.sync.dma_start(wa_raw[0][:], wa_rows[:, :, half(0)])
-        for q in range(4):
-            nc.sync.dma_start(
-                table_scales[32 * q : 32 * q + 4, :].bitcast(I32), x_scales[0, 4 * q : 4 * q + 4, :].bitcast(I32)
-            )
+        for r in range(4):
+            nc.sync.dma_start(table_scales[r:P:32, :].bitcast(I32), x_scales[0, r:16:4, :].bitcast(I32))
         table_words = sbuf("table_words", [P, T], I32)
         nc.sync.dma_start(table_words[:], x_words[0].rearrange("p n t -> p (n t)").bitcast(I32))
         nc.sync.dma_start(wa_raw[1][:], wa_rows[:, :, half(1)])
@@ -101,113 +99,107 @@ def tile_picked_toklapwsum_none_p_kernel(
             token_words[:].rearrange("p t m -> p m t"), table_words[:].bitcast(U32).indirect(picks[:])
         )
 
-        gy = [sbuf("gy%d" % t, [P, H], F32) for t in range(PACK)]
         y_acc = {}
         for h in range(HALVES):
             grouped = sbuf("wa_grouped%d" % h, [P, W, PACK], BF16)
             if h == 0:
                 interleave(nc.scalar.copy, grouped[:], wa_raw[h][:])
             else:
-                cut = 160
-                interleave(nc.vector.tensor_copy, grouped[:, :cut, :], wa_raw[h][:, :, :cut])
-                interleave(nc.scalar.copy, grouped[:, cut:, :], wa_raw[h][:, :, cut:])
+                interleave(nc.vector.tensor_copy, grouped[:, :WA_VECTOR_COLS, :], wa_raw[h][:, :, :WA_VECTOR_COLS])
+                interleave(nc.scalar.copy, grouped[:, WA_VECTOR_COLS:, :], wa_raw[h][:, :, WA_VECTOR_COLS:])
             wa_q = quantize("wa%d" % h, grouped[:].rearrange("p c j -> p (c j)"), W)
             for t in range(PACK):
                 y_acc[t, h] = product("y%d_%d" % (t, h), token_words[:, t, :], token_scales[:, t, :], wa_q)
 
-        w1_grouped = sbuf("w1_grouped", [P, PACK, P, PACK], BF16)
-        half_window = [sbuf("half_window%d" % t, [P, 2 * H], F32) for t in range(PACK)]
-        tanh_window = [sbuf("tanh_window%d" % t, [P, 2 * H], F32) for t in range(PACK)]
-        half_h = [tile[:, :H] for tile in half_window]
-        tanh_h = [tile[:, :H] for tile in tanh_window]
-        firsts = {}
-
-        def weigh_on_scalar(t, h):
-            nc.scalar.activation(gy[t][:, half(h)], y_acc[t, h][:], ACT.Copy, scale=gains[:, t : t + 1])
-
-        def weigh_on_vector(t, h):
-            nc.vector.tensor_scalar(gy[t][:, half(h)], y_acc[t, h][:], gains[:, t : t + 1], None, ALU.mult)
-
-        def look_up_first(t, h):
-            first = tanh_window[t][:, H + h * W : H + (h + 1) * W]
-            nc.scalar.activation(first, gy[t][:].indirect(entries(list1, h)), ACT.Copy)
-            firsts[t, h] = first
-
-        def cast_w1():
-            for g in range(2):
-                ms = slice(g * P // 2, (g + 1) * P // 2)
-                nc.scalar.copy(
-                    w1_grouped[:, :, ms, :].rearrange("p t m j -> p m j t"),
-                    w1_raw[:].rearrange("p j (m t) -> p m j t", t=PACK)[:, ms, :, :],
-                )
-
+        gy = [sbuf("gy%d" % t, [P, H], F32) for t in range(PACK)]
+        at_n1 = [sbuf("at_n1_%d" % t, [P, H], F32) for t in range(PACK)]
+        pair_sum = [sbuf("pair_sum%d" % t, [P, H], F32) for t in range(PACK)]
         z_planes = [sbuf("z_planes%d" % h, [P, PACK, W], BF16) for h in range(HALVES)]
         z_grouped = [sbuf("z_grouped%d" % h, [P, W, PACK], BF16) for h in range(HALVES)]
-        pair_sums = {}
+        z_steps = [(0, 0), (0, 1)] + [(t, h) for h in range(HALVES) for t in range(1, PACK)]
 
-        def add_second(t, h):
-            both = half_window[t][:, H:][:, half(h)]
-            nc.vector.tensor_tensor(both, gy[t][:].indirect(entries(list2, h)), firsts[t, h], ALU.add)
-            pair_sums[t, h] = both
+        for t, h in z_steps:
+            if h == 0:
+                nc.scalar.activation(gy[t][:, half(0)], y_acc[t, 0][:], ACT.Copy, scale=gains[:, t : t + 1])
+                nc.vector.tensor_scalar(gy[t][:, half(1)], y_acc[t, 1][:], gains[:, t : t + 1], None, ALU.mult)
+            nc.scalar.activation(at_n1[t][:, half(h)], gy[t][:].indirect(entries(list1, half(h))), ACT.Copy)
+
+        w1_grouped = sbuf("w1_grouped", [P, PACK, P, PACK], BF16)
+        for g in range(2):
+            ms = slice(g * P // 2, (g + 1) * P // 2)
+            nc.scalar.copy(
+                w1_grouped[:, :, ms, :].rearrange("p t m j -> p m j t"),
+                w1_raw[:].rearrange("p j (m t) -> p m j t", t=PACK)[:, ms, :, :],
+            )
+
+        def add_n2(t, h):
+            nc.vector.tensor_tensor(
+                pair_sum[t][:, half(h)], gy[t][:].indirect(entries(list2, half(h))), at_n1[t][:, half(h)], ALU.add
+            )
 
         def finish_z(t, h):
             nc.vector.scalar_tensor_tensor(
-                z_planes[h][:, t, :], pair_sums[t, h], 0.75, gy[t][:, half(h)], ALU.mult, ALU.subtract
+                z_planes[h][:, t, :], pair_sum[t][:, half(h)], 0.75, gy[t][:, half(h)], ALU.mult, ALU.subtract
             )
 
+        add_n2(*z_steps[0])
+        for previous, step in zip(z_steps, z_steps[1:]):
+            add_n2(*step)
+            finish_z(*previous)
+        interleave(nc.scalar.copy, z_grouped[0][:], z_planes[0][:])
+        w1_codes, w1_scales = quantize("w1", w1_grouped[:].rearrange("p t m j -> p (t m j)"), N)
+        finish_z(*z_steps[-1])
+
+        half_h = [sbuf("half_h%d" % t, [P, H], F32) for t in range(PACK)]
+        tanh_h = [sbuf("tanh_h%d" % t, [P, H], F32) for t in range(PACK)]
         h_acc = {}
 
-        def second_product(h, z_q, w1_q):
+        def second_product(h):
+            z_q = quantize("z%d" % h, z_grouped[h][:].rearrange("p c j -> p (c j)"), W)
             for t in range(PACK):
                 cols = slice(t * P, (t + 1) * P)
-                h_acc[t, h] = product("h%d_%d" % (t, h), w1_q[0][:, cols], w1_q[1][:, cols], z_q)
-                if h == 0 or t == 0:
-                    nc.scalar.activation(tanh_h[t][:, half(h)], h_acc[t, h][:], ACT.Tanh, scale=0.5)
+                h_acc[t, h] = product("h%d_%d" % (t, h), w1_codes[:, cols], w1_scales[:, cols], z_q)
 
-        for t in range(PACK):
-            weigh_on_scalar(t, 0)
-            weigh_on_vector(t, 1)
-            look_up_first(t, 0)
-        for t in range(PACK):
-            look_up_first(t, 1)
-        cast_w1()
+        def take_tanh(t, h):
+            nc.scalar.activation(tanh_h[t][:, half(h)], h_acc[t, h][:], ACT.Tanh, scale=0.5)
 
-        steps = [(t, h) for h in range(HALVES) for t in range(PACK)]
-        for i, step in enumerate(steps):
-            add_second(*step)
-            if i > 0:
-                finish_z(*steps[i - 1])
-        finish_z(*steps[-1])
-        interleave(nc.scalar.copy, z_grouped[0][:], z_planes[0][:])
-        w1_q = quantize("w1", w1_grouped[:].rearrange("p t m j -> p (t m j)"), N)
-        z_q0 = quantize("z0", z_grouped[0][:].rearrange("p c j -> p (c j)"), W)
-        second_product(0, z_q0, w1_q)
+        def take_half(t, h):
+            nc.vector.tensor_scalar(half_h[t][:, half(h)], h_acc[t, h][:], 0.5, None, ALU.mult)
+
+        second_product(0)
+        for t in range(PACK):
+            take_tanh(t, 0)
         interleave(nc.vector.tensor_copy, z_grouped[1][:], z_planes[1][:])
-        z_q1 = quantize("z1", z_grouped[1][:].rearrange("p c j -> p (c j)"), W)
-        second_product(1, z_q1, w1_q)
+        second_product(1)
         for t in range(PACK):
-            for h in range(HALVES):
-                nc.vector.tensor_scalar(half_h[t][:, half(h)], h_acc[t, h][:], 0.5, None, ALU.mult)
+            take_half(t, 0)
+        for t in range(PACK):
+            take_tanh(t, 1)
+            take_half(t, 1)
 
         out_rows = out.rearrange("(p t) n -> p t n", t=PACK)
-        right = sbuf("right", [P, H], F32)
-        for t in range(PACK):
-            if t > 0:
-                nc.scalar.activation(tanh_h[t][:, half(1)], half_h[t][:, half(1)], ACT.Tanh)
-            gate = sbuf("gate%d" % t, [P, H], F32)
-            third = sbuf("third%d" % t, [P, H], F32)
-            left = sbuf("left%d" % t, [P, H], F32)
-            result = sbuf("result%d" % t, [P, H], F32)
-            whole = [(slice(0, H), slice(0, H // 16))]
-            halves = [(half(h), slice(h * LIST_COLS, (h + 1) * LIST_COLS)) for h in range(HALVES)]
-            for cols, part in halves if t == PACK - 1 else whole:
-                nc.scalar.activation(gate[:, cols], tanh_window[t][:].indirect(list5[:, part]), ACT.Copy, bias=1.0)
-            for cols, part in halves if t == PACK - 1 else whole:
-                nc.vector.tensor_tensor(right[:, cols], half_window[t][:].indirect(list4[:, part]), gate[:, cols], ALU.mult)
-            for cols, part in halves if t == PACK - 1 else whole:
-                nc.scalar.activation(third[:, cols], half_window[t][:].indirect(list3[:, part]), ACT.Copy)
-                nc.vector.scalar_tensor_tensor(left[:, cols], tanh_h[t][:, cols], 1.0, third[:, cols], ALU.add, ALU.mult)
-            for cols, part in halves if t == PACK - 1 else whole:
-                nc.vector.tensor_tensor(result[:, cols], left[:, cols], right[:, cols], ALU.add)
-                nc.sync.dma_start(out_rows[:, t, cols], result[:, cols])
-            right = third
+        gate = [sbuf("gate%d" % t, [P, H], F32) for t in range(PACK)]
+        at_n3 = [sbuf("at_n3_%d" % t, [P, H], F32) for t in range(PACK)]
+        left = [sbuf("left%d" % t, [P, H], F32) for t in range(PACK)]
+        right = [sbuf("right%d" % t, [P, H], F32) for t in range(PACK)]
+        result = [sbuf("result%d" % t, [P, H], F32) for t in range(PACK)]
+
+        def make_terms(t, cols):
+            nc.scalar.activation(gate[t][:, cols], tanh_h[t][:].indirect(entries(list5, cols)), ACT.Copy, bias=1.0)
+            nc.scalar.activation(at_n3[t][:, cols], half_h[t][:].indirect(entries(list3, cols)), ACT.Copy)
+            nc.vector.tensor_tensor(right[t][:, cols], half_h[t][:].indirect(entries(list4, cols)), gate[t][:, cols], ALU.mult)
+            nc.vector.scalar_tensor_tensor(left[t][:, cols], tanh_h[t][:, cols], 1.0, at_n3[t][:, cols], ALU.add, ALU.mult)
+
+        def add_and_store(t, cols):
+            nc.vector.tensor_tensor(result[t][:, cols], left[t][:, cols], right[t][:, cols], ALU.add)
+            if t == PACK - 1:
+                nc.sync.dma_start(out_rows[:, t, cols], result[t][:, cols])
+            elif cols.stop == H:
+                nc.sync.dma_start(out_rows[:, t, :], result[t][:])
+
+        out_steps = [(t, half(h)) for t in range(PACK) for h in range(HALVES)]
+        make_terms(*out_steps[0])
+        for previous, step in zip(out_steps, out_steps[1:]):
+            make_terms(*step)
+            add_and_store(*previous)
+        add_and_store(*out_steps[-1])

from contextlib import ExitStack

import concourse.mybir as mybir

K, T, S, N, H = 512, 2048, 512, 512, 512
FLOPS = 2 * K * S * H + 2 * S * N * H

F32 = mybir.dt.float32
BF16 = mybir.dt.bfloat16
I32 = mybir.dt.int32
U32 = mybir.dt.uint32
U16 = mybir.dt.uint16
U8 = mybir.dt.uint8
FP8X4 = mybir.dt.float8_e4m3fn_x4
ALU = mybir.AluOpType
ACT = mybir.ActivationFunctionType

P = 128
PACK = 4
HALVES = 2
W = H // HALVES
WA_VECTOR_COLS = 160


def tile_picked_toklapwsum_none_p_kernel(
    tc, x_words, x_scales, wa, gt, w1, offs, n1, n2, n3, n4, n5, out
):
    nc = tc.nc
    with ExitStack() as ctx:
        held = ctx.enter_context(tc.tile_pool(name="held", bufs=1))
        psum = ctx.enter_context(tc.psum_pool(name="psum", bufs=8))

        def sbuf(name, shape, dtype):
            return held.tile(shape, dtype, name=name, align_bytes=64)

        def load_list(name, source):
            tile = held.tile([P, S // 16], U16, name=name)
            nc.sync.dma_start(tile[:], source)
            return tile

        def half(h):
            return slice(h * W, (h + 1) * W)

        def entries(tile, cols):
            return tile[:, cols.start // 16 : cols.stop // 16]

        def interleave(copy, grouped, planes):
            copy(
                grouped.rearrange("p (c i) j -> p c j i", i=4),
                planes.rearrange("p j (c i) -> p c j i", i=4),
            )

        def quantize(name, grouped, width):
            codes = sbuf(name + "_codes", [P, width], U32)
            scales = sbuf(name + "_scales", [P, width], U8)
            nc.vector.quantize_mx(out=codes[:].bitcast(FP8X4), scales=scales[:], in_=grouped)
            return codes, scales

        def product(name, lhs_codes, lhs_scales, rhs):
            acc = psum.tile([P, W], F32, name=name, tag="acc")
            nc.tensor.matmul_mx(
                out=acc[:],
                lhsT=lhs_codes.bitcast(FP8X4),
                lhsT_scale=lhs_scales,
                rhs=rhs[0][:].bitcast(FP8X4),
                rhs_scale=rhs[1][:],
                start=True,
                stop=True,
            )
            return acc

        table_scales = sbuf("table_scales", [P, T], U8)
        nc.vector.memset(table_scales[:].bitcast(I32), 0)
        picks = load_list("picks", offs)
        wa_rows = wa.rearrange("(p j) n -> p j n", j=PACK)
        wa_raw = [sbuf("wa_raw%d" % h, [P, PACK, W], F32) for h in range(HALVES)]
        nc.sync.dma_start(wa_raw[0][:], wa_rows[:, :, half(0)])
        for r in range(4):
            nc.sync.dma_start(table_scales[r:P:32, :].bitcast(I32), x_scales[0, r:16:4, :].bitcast(I32))
        table_words = sbuf("table_words", [P, T], I32)
        nc.sync.dma_start(table_words[:], x_words[0].rearrange("p n t -> p (n t)").bitcast(I32))
        nc.sync.dma_start(wa_raw[1][:], wa_rows[:, :, half(1)])
        gains = sbuf("gains", [P, PACK], F32)
        nc.sync.dma_start(gains[:], gt.rearrange("(p t) o -> p (t o)", t=PACK))
        list1 = load_list("list1", n1)
        list2 = load_list("list2", n2)
        w1_raw = sbuf("w1_raw", [P, PACK, N], F32)
        nc.sync.dma_start(w1_raw[:], w1.rearrange("(p j) n -> p j n", j=PACK))
        list5 = load_list("list5", n5)
        list3 = load_list("list3", n3)
        list4 = load_list("list4", n4)

        picked_scales = sbuf("picked_scales", [P, S], U8)
        nc.vector.tensor_copy(picked_scales[:], table_scales[:].indirect(picks[:]))
        token_scales = sbuf("token_scales", [P, PACK, P], U8)
        nc.vector.tensor_copy(token_scales[:], picked_scales[:].rearrange("p (m t) -> p t m", t=PACK))
        token_words = sbuf("token_words", [P, PACK, P], U32)
        nc.vector.tensor_copy(
            token_words[:].rearrange("p t m -> p m t"), table_words[:].bitcast(U32).indirect(picks[:])
        )

        y_acc = {}
        for h in range(HALVES):
            grouped = sbuf("wa_grouped%d" % h, [P, W, PACK], BF16)
            if h == 0:
                interleave(nc.scalar.copy, grouped[:], wa_raw[h][:])
            else:
                interleave(nc.vector.tensor_copy, grouped[:, :WA_VECTOR_COLS, :], wa_raw[h][:, :, :WA_VECTOR_COLS])
                interleave(nc.scalar.copy, grouped[:, WA_VECTOR_COLS:, :], wa_raw[h][:, :, WA_VECTOR_COLS:])
            wa_q = quantize("wa%d" % h, grouped[:].rearrange("p c j -> p (c j)"), W)
            for t in range(PACK):
                y_acc[t, h] = product("y%d_%d" % (t, h), token_words[:, t, :], token_scales[:, t, :], wa_q)

        gy = [sbuf("gy%d" % t, [P, H], F32) for t in range(PACK)]
        at_n1 = [sbuf("at_n1_%d" % t, [P, H], F32) for t in range(PACK)]
        pair_sum = [sbuf("pair_sum%d" % t, [P, H], F32) for t in range(PACK)]
        z_planes = [sbuf("z_planes%d" % h, [P, PACK, W], BF16) for h in range(HALVES)]
        z_grouped = [sbuf("z_grouped%d" % h, [P, W, PACK], BF16) for h in range(HALVES)]
        z_steps = [(0, 0), (0, 1)] + [(t, h) for h in range(HALVES) for t in range(1, PACK)]

        for t, h in z_steps:
            if h == 0:
                nc.scalar.activation(gy[t][:, half(0)], y_acc[t, 0][:], ACT.Copy, scale=gains[:, t : t + 1])
                nc.vector.tensor_scalar(gy[t][:, half(1)], y_acc[t, 1][:], gains[:, t : t + 1], None, ALU.mult)
            nc.scalar.activation(at_n1[t][:, half(h)], gy[t][:].indirect(entries(list1, half(h))), ACT.Copy)

        w1_grouped = sbuf("w1_grouped", [P, PACK, P, PACK], BF16)
        for g in range(2):
            ms = slice(g * P // 2, (g + 1) * P // 2)
            nc.scalar.copy(
                w1_grouped[:, :, ms, :].rearrange("p t m j -> p m j t"),
                w1_raw[:].rearrange("p j (m t) -> p m j t", t=PACK)[:, ms, :, :],
            )

        def add_n2(t, h):
            nc.vector.tensor_tensor(
                pair_sum[t][:, half(h)], gy[t][:].indirect(entries(list2, half(h))), at_n1[t][:, half(h)], ALU.add
            )

        def finish_z(t, h):
            nc.vector.scalar_tensor_tensor(
                z_planes[h][:, t, :], pair_sum[t][:, half(h)], 0.75, gy[t][:, half(h)], ALU.mult, ALU.subtract
            )

        add_n2(*z_steps[0])
        for previous, step in zip(z_steps, z_steps[1:]):
            add_n2(*step)
            finish_z(*previous)
        interleave(nc.scalar.copy, z_grouped[0][:], z_planes[0][:])
        w1_codes, w1_scales = quantize("w1", w1_grouped[:].rearrange("p t m j -> p (t m j)"), N)
        finish_z(*z_steps[-1])

        half_h = [sbuf("half_h%d" % t, [P, H], F32) for t in range(PACK)]
        tanh_h = [sbuf("tanh_h%d" % t, [P, H], F32) for t in range(PACK)]
        h_acc = {}

        def second_product(h):
            z_q = quantize("z%d" % h, z_grouped[h][:].rearrange("p c j -> p (c j)"), W)
            for t in range(PACK):
                cols = slice(t * P, (t + 1) * P)
                h_acc[t, h] = product("h%d_%d" % (t, h), w1_codes[:, cols], w1_scales[:, cols], z_q)

        def take_tanh(t, h):
            nc.scalar.activation(tanh_h[t][:, half(h)], h_acc[t, h][:], ACT.Tanh, scale=0.5)

        def take_half(t, h):
            nc.vector.tensor_scalar(half_h[t][:, half(h)], h_acc[t, h][:], 0.5, None, ALU.mult)

        second_product(0)
        for t in range(PACK):
            take_tanh(t, 0)
        interleave(nc.vector.tensor_copy, z_grouped[1][:], z_planes[1][:])
        second_product(1)
        for t in range(PACK):
            take_half(t, 0)
        for t in range(PACK):
            take_tanh(t, 1)
            take_half(t, 1)

        out_rows = out.rearrange("(p t) n -> p t n", t=PACK)
        gate = [sbuf("gate%d" % t, [P, H], F32) for t in range(PACK)]
        at_n3 = [sbuf("at_n3_%d" % t, [P, H], F32) for t in range(PACK)]
        left = [sbuf("left%d" % t, [P, H], F32) for t in range(PACK)]
        right = [sbuf("right%d" % t, [P, H], F32) for t in range(PACK)]
        result = [sbuf("result%d" % t, [P, H], F32) for t in range(PACK)]

        def make_terms(t, cols):
            nc.scalar.activation(gate[t][:, cols], tanh_h[t][:].indirect(entries(list5, cols)), ACT.Copy, bias=1.0)
            nc.scalar.activation(at_n3[t][:, cols], half_h[t][:].indirect(entries(list3, cols)), ACT.Copy)
            nc.vector.tensor_tensor(right[t][:, cols], half_h[t][:].indirect(entries(list4, cols)), gate[t][:, cols], ALU.mult)
            nc.vector.scalar_tensor_tensor(left[t][:, cols], tanh_h[t][:, cols], 1.0, at_n3[t][:, cols], ALU.add, ALU.mult)

        def add_and_store(t, cols):
            nc.vector.tensor_tensor(result[t][:, cols], left[t][:, cols], right[t][:, cols], ALU.add)
            if t == PACK - 1:
                nc.sync.dma_start(out_rows[:, t, cols], result[t][:, cols])
            elif cols.stop == H:
                nc.sync.dma_start(out_rows[:, t, :], result[t][:])

        out_steps = [(t, half(h)) for t in range(PACK) for h in range(HALVES)]
        make_terms(*out_steps[0])
        for previous, step in zip(out_steps, out_steps[1:]):
            make_terms(*step)
            add_and_store(*previous)
        add_and_store(*out_steps[-1])
